import numpy as np
import ml_dtypes


def mxq(x, axis, fmt="e4m3"):
    dtype, down = {"e4m3": (ml_dtypes.float8_e4m3fn, 7), "e5m2": (ml_dtypes.float8_e5m2, 14)}[fmt]
    v = np.moveaxis(np.asarray(x, np.float32).astype(ml_dtypes.bfloat16).astype(np.float64), axis, -1)
    blocks = v.reshape(v.shape[:-1] + (-1, 32))
    amax = np.abs(blocks).max(-1, keepdims=True)
    byte = np.maximum(np.where(amax > 0, np.frexp(amax)[1] - 1 + 127, 0) - down, 1)
    scale = np.exp2(byte - 127.0)
    codes = (blocks / scale).astype(np.float32).astype(dtype).astype(np.float64)
    return np.moveaxis((codes * scale).reshape(v.shape), -1, axis)


WIDE = False


def mx_kscale(k):
    if not WIDE:
        return np.ones(k)
    levels = np.array([10, -10, 5, -5, 0])
    if k % 512:
        return np.exp2(np.random.permutation(np.resize(levels, k // 32))).repeat(32)
    a = np.empty((k // 512, 16))
    for p in range(k // 512):
        a[p, :8] = np.random.permutation(np.resize(levels, 8))
        for g in range(8):
            far = levels[np.abs(levels - a[p, g]) >= 10]
            a[p, g + 8] = far[np.random.randint(len(far))]
    return np.exp2(a.ravel()).repeat(32)


def f64(x):
    return np.asarray(x).astype(np.float64)


def striped(idx):
    return np.tile(idx.reshape(-1, 16).T, (8, 1)).astype(np.uint16)


def unstriped(offs):
    return offs[:16].T.reshape(-1).astype(np.int64)


E2M1 = np.array([0.0, 0.5, 1.0, 1.5, 2.0, 3.0, 4.0, 6.0, -0.0, -0.5, -1.0, -1.5, -2.0, -3.0, -4.0, -6.0])


def pack_weight(w, fmt):
    k, n = w.shape
    w = f64(np.asarray(w, np.float32).astype(ml_dtypes.bfloat16)).reshape(k // 32, 32, n)
    amax = np.abs(w).max(1)
    if fmt == "e4m3":
        byte = np.frexp(amax)[1] - 1 + 127 - 7
    else:
        mant, ex = np.frexp(amax / 6.0)
        byte = np.where(mant > 0.5, ex, ex - 1) + 127
    byte = np.clip(np.where(amax > 0, byte, 1), 1, 254)
    scaled = (w * np.exp2(127.0 - byte)[:, None, :]).reshape(k, n).astype(np.float32)
    by_word = np.ascontiguousarray(scaled.reshape(k // 512, 128, 4, n).transpose(0, 1, 3, 2))
    if fmt == "e4m3":
        words = by_word.astype(ml_dtypes.float8_e4m3fn).view(np.uint8)
    else:
        c = by_word.astype(ml_dtypes.float4_e2m1fn).view(np.uint8) & 0xF
        words = (c[..., 0::2] | (c[..., 1::2] << 4)).reshape(k // 512, 128, 2 * n)
    return np.ascontiguousarray(words), np.ascontiguousarray(byte.astype(np.uint8).reshape(k // 512, 16, n))


def unpack_weight(words, scales, fmt):
    g, _, n = scales.shape
    words = np.ascontiguousarray(words).reshape(g, 128, n, -1)
    if fmt == "e4m3":
        vals = words.view(ml_dtypes.float8_e4m3fn).astype(np.float64)
    else:
        nib = np.empty((g, 128, n, 4), np.uint8)
        nib[..., 0::2] = words & 0xF
        nib[..., 1::2] = words >> 4
        vals = E2M1[nib]
    vals = vals * np.repeat(np.exp2(scales.astype(np.float64) - 127.0), 8, axis=1)[..., None]
    return vals.transpose(0, 1, 3, 2).reshape(g * 512, n)


def gelu(v):
    return 0.5 * v * (1.0 + np.tanh(np.sqrt(2.0 / np.pi) * (v + 0.044715 * v**3)))


K, H, N, T, S = 1024, 1024, 512, 4096, 1024

def setup_inputs():
    n = np.random.standard_normal
    s = mx_kscale(K)[:, None]
    u = mx_kscale(H)[:, None]
    tab_words, tab_scales = pack_weight(n((K, T)) * s, "e4m3")
    w4_words, w4_scales = pack_weight(0.5 * n((H, N)) / np.sqrt(H) / u, "e2m1")
    return {
        "tab_words": tab_words, "tab_scales": tab_scales,
        "offs": striped(np.random.permutation(T)[:S]),
        "w1": (n((K, H)) / np.sqrt(K) / s * u.T).astype(np.float32),
        "stiff": (0.5 * np.exp(0.3 * n((H, S))) / u).astype(np.float32),
        "w4_words": w4_words, "w4_scales": w4_scales,
        "offs2": striped(np.random.permutation(S)),
        "wgo": np.exp(0.3 * n((128, S))).astype(np.float32),
        "x0": n((N, S)).astype(np.float32),
    }

def reference(tab_words, tab_scales, offs, w1, stiff, w4_words, w4_scales, offs2, wgo, x0):
    v = unpack_weight(tab_words, tab_scales, "e4m3")[:, unstriped(offs)]
    d = mxq(f64(w1), 0, "e4m3").T @ v
    h = d + f64(stiff) * np.square(d)
    w4 = unpack_weight(w4_words, w4_scales, "e2m1")
    y = w4.T @ mxq(h, 0, "e4m3")
    page = np.zeros((N, S))
    page[:, unstriped(offs2)] = np.tile(f64(wgo), (N // 128, 1)) * y
    return f64(x0) * (1.0 - page)

@@ -1,0 +1,264 @@
+from contextlib import ExitStack
+
+import concourse.mybir as mybir
+
+K, H, N, T, S = 1024, 1024, 512, 4096, 1024
+FLOPS = 2 * K * H * S + 2 * H * N * S
+
+F32 = mybir.dt.float32
+BF16 = mybir.dt.bfloat16
+I32 = mybir.dt.int32
+U32 = mybir.dt.uint32
+U16 = mybir.dt.uint16
+U8 = mybir.dt.uint8
+FP8X4 = mybir.dt.float8_e4m3fn_x4
+FP4X4 = mybir.dt.float4_e2m1fn_x4
+MULT = mybir.AluOpType.mult
+ADD = mybir.AluOpType.add
+COPY = mybir.ActivationFunctionType.Copy
+
+P = 128
+PACK = 4
+KP = P * PACK
+CHUNK = 256
+BANK_J = 128
+
+
+def tile_list_kidney_mesh_stress_kernel(
+    tc, tab_words, tab_scales, offs, w1, stiff, w4_words, w4_scales, offs2, wgo, x0, out
+):
+    nc = tc.nc
+    n_chunks = S // CHUNK
+
+    with ExitStack() as ctx:
+        keep = ctx.enter_context(tc.tile_pool(name="keep", bufs=1))
+        ring = ctx.enter_context(tc.tile_pool(name="ring", bufs=3))
+        psum_d = ctx.enter_context(tc.psum_pool(name="psum_d", bufs=5))
+        psum_y = ctx.enter_context(tc.psum_pool(name="psum_y", bufs=3))
+
+        offs_sb = keep.tile([P, S // 16], U16, name="offs_sb")
+        offs2_sb = keep.tile([P, S // 16], U16, name="offs2_sb")
+
+        tab_sc = keep.tile([P, T], U8, name="tab_sc", align_bytes=64)
+        w4_sc = keep.tile([P, 2, N], U8, name="w4_sc", align_bytes=64)
+        nc.gpsimd.memset(tab_sc[:].bitcast(I32), 0)
+        for q in range(4):
+            nc.gpsimd.dma_start(
+                out=tab_sc[32 * q : 32 * q + 8, :].bitcast(I32),
+                in_=tab_scales[:, 4 * q : 4 * q + 4, :].bitcast(I32),
+            )
+        nc.gpsimd.memset(w4_sc[:].rearrange("p a n -> p (a n)").bitcast(I32), 0)
+        for q in range(4):
+            nc.gpsimd.dma_start(
+                out=w4_sc[32 * q : 32 * q + 4, :, :].bitcast(I32),
+                in_=w4_scales[:, 4 * q : 4 * q + 4, :].rearrange("a r n -> r a n").bitcast(I32),
+            )
+
+        w1_raw = {}
+        w1_codes = {}
+        w1_sc = {}
+        stiff_sb = {}
+        tab_sb = {}
+        h_codes = {}
+        h_sc = {}
+
+        def load_w1(a, b):
+            raw = keep.tile([P, PACK, KP], F32, name=f"w1_raw{a}{b}")
+            nc.sync.dma_start(
+                out=raw[:],
+                in_=w1[KP * a : KP * (a + 1), KP * b : KP * (b + 1)].rearrange("(p j) c -> p j c", j=PACK),
+            )
+            w1_raw[a, b] = raw
+
+        def load_tab(a):
+            words = keep.tile([P, T], U32, name=f"tab{a}")
+            nc.sync.dma_start(
+                out=words[:].bitcast(I32),
+                in_=tab_words[a].rearrange("p n t -> p (n t)").bitcast(I32),
+            )
+            tab_sb[a] = words
+
+        def load_stiff(b, c):
+            st = keep.tile([P, PACK, CHUNK], F32, name=f"stiff{b}{c}")
+            nc.sync.dma_start(
+                out=st[:],
+                in_=stiff[KP * b : KP * (b + 1), CHUNK * c : CHUNK * (c + 1)].rearrange("(p t) j -> p t j", t=PACK),
+            )
+            stiff_sb[b, c] = st
+
+        nc.sync.dma_start(offs_sb[:], offs)
+        load_w1(0, 0)
+        load_w1(1, 0)
+        load_tab(0)
+        load_tab(1)
+        load_stiff(0, 0)
+        load_stiff(0, 1)
+        load_w1(0, 1)
+        load_stiff(0, 2)
+        load_w1(1, 1)
+        load_stiff(1, 0)
+        w4_sb = keep.tile([P, 2, 2 * N], U8, name="w4_sb", align_bytes=64)
+        nc.sync.dma_start(out=w4_sb[:].bitcast(I32), in_=w4_words.rearrange("a p n -> p a n").bitcast(I32))
+        nc.sync.dma_start(offs2_sb[:], offs2)
+        wgo_sb = keep.tile([P, S], F32, name="wgo_sb")
+        nc.sync.dma_start(out=wgo_sb[:], in_=wgo)
+        load_stiff(1, 1)
+        load_stiff(1, 2)
+        load_stiff(0, 3)
+        load_stiff(1, 3)
+        x0_sb = []
+        for q in range(4):
+            xt = keep.tile([P, S], F32, name=f"x0_{q}")
+            nc.sync.dma_start(out=xt[:], in_=x0[P * q : P * (q + 1), :])
+            x0_sb.append(xt)
+
+        def quantise_w1(a, b):
+            grouped = ring.tile([P, KP * PACK], BF16, name="w1_bf", align_bytes=64, bufs=2)
+            nc.scalar.copy(
+                out=grouped[:].rearrange("p (th tl m j) -> p th m j tl", th=2, tl=2, j=PACK),
+                in_=w1_raw[a, b][:].rearrange("p j (m th tl) -> p th m j tl", th=2, tl=2),
+            )
+            codes = keep.tile([P, KP], U32, name=f"w1_codes{a}{b}", align_bytes=64)
+            sc = keep.tile([P, KP], U8, name=f"w1_sc{a}{b}", align_bytes=64)
+            nc.vector.quantize_mx(out=codes[:].bitcast(FP8X4), scales=sc[:], in_=grouped[:])
+            w1_codes[a, b] = codes
+            w1_sc[a, b] = sc
+
+        v_words = {}
+
+        def gather_words(a, half):
+            picked = keep.tile([P, S // 2], U32, name=f"v_words{a}{half}", align_bytes=64)
+            nc.vector.tensor_copy(picked[:], tab_sb[a][:].indirect(offs_sb[:, 32 * half : 32 * (half + 1)]))
+            v_words[a, half] = picked
+
+        quantise_w1(0, 0)
+        v_sc = keep.tile([P, S], U8, name="v_sc", align_bytes=64)
+        nc.vector.tensor_copy(v_sc[:], tab_sc[:].indirect(offs_sb[:]))
+        quantise_w1(1, 0)
+        gather_words(0, 0)
+        gather_words(0, 1)
+        gather_words(1, 0)
+
+        def make_h(b, c):
+            h_bf = ring.tile([P, CHUNK * PACK], BF16, name="h_bf", align_bytes=64)
+            banks = []
+            us = []
+            for s in range(CHUNK // BANK_J):
+                j0 = CHUNK * c + BANK_J * s
+                half, jh = divmod(j0, S // 2)
+                bank = psum_d.tile([P, PACK, BANK_J], F32, name="d_bank")
+                for t in range(PACK):
+                    for a in range(2):
+                        nc.tensor.matmul_mx(
+                            out=bank[:, t, :],
+                            lhsT=w1_codes[a, b][:, P * t : P * (t + 1)].bitcast(FP8X4),
+                            lhsT_scale=w1_sc[a, b][:, P * t : P * (t + 1)],
+                            rhs=v_words[a, half][:, jh : jh + BANK_J].bitcast(FP8X4),
+                            rhs_scale=v_sc[4 * a :, j0 : j0 + BANK_J],
+                            start=(a == 0),
+                            stop=(a == 1),
+                        )
+                u = ring.tile([P, BANK_J * PACK], F32, name="u", bufs=4)
+                nc.vector.tensor_tensor(
+                    u[:].rearrange("p (c i t) -> p c t i", i=2, t=PACK),
+                    bank[:].rearrange("p t (c i) -> p c t i", i=2),
+                    stiff_sb[b, c][:, :, BANK_J * s : BANK_J * (s + 1)].rearrange("p t (c i) -> p c t i", i=2),
+                    MULT,
+                )
+                banks.append(bank)
+                us.append(u)
+            for s in range(CHUNK // BANK_J):
+                nc.vector.scalar_tensor_tensor(
+                    h_bf[:, BANK_J * PACK * s : BANK_J * PACK * (s + 1)].rearrange("p (j t) -> p j t", t=PACK),
+                    us[s][:].rearrange("p (j t) -> p j t", t=PACK),
+                    1.0,
+                    banks[s][:].rearrange("p t j -> p j t"),
+                    ADD,
+                    MULT,
+                )
+            return h_bf
+
+        def quantise_h(b, c, h_bf):
+            codes = keep.tile([P, CHUNK], U32, name=f"h_codes{b}{c}", align_bytes=64)
+            sc = keep.tile([P, CHUNK], U8, name=f"h_sc{b}{c}", align_bytes=64)
+            nc.vector.quantize_mx(out=codes[:].bitcast(FP8X4), scales=sc[:], in_=h_bf[:])
+            h_codes[b, c] = codes
+            h_sc[b, c] = sc
+
+        pages = [keep.tile([P, S], F32, name=f"page{q}") for q in range(4)]
+
+        def make_y(c):
+            ys = []
+            for pair in range(2):
+                bank = psum_y.tile([P, 2, CHUNK], F32, name="y_bank")
+                for qq in range(2):
+                    q = 2 * pair + qq
+                    for s in range(CHUNK // BANK_J):
+                        cols = slice(BANK_J * s, BANK_J * (s + 1))
+                        for b in range(2):
+                            nc.tensor.matmul_mx(
+                                out=bank[:, qq, cols],
+                                lhsT=w4_sb[:, b, 2 * P * q : 2 * P * (q + 1)].bitcast(FP4X4),
+                                lhsT_scale=w4_sc[:, b, P * q : P * (q + 1)],
+                                rhs=h_codes[b, c][:, cols].bitcast(FP8X4),
+                                rhs_scale=h_sc[b, c][:, cols],
+                                start=(b == 0),
+                                stop=(b == 1),
+                            )
+                y_neg = ring.tile([P, 2, CHUNK], F32, name="y_neg", bufs=4)
+                nc.scalar.activation(y_neg[:], bank[:], COPY, scale=-1.0)
+                ys.append(y_neg)
+            return ys
+
+        def scatter(c, q, ys):
+            nc.vector.tensor_tensor(
+                pages[q][:].indirect(offs2_sb[:, 16 * c : 16 * (c + 1)]),
+                ys[q // 2][:, q % 2, :],
+                wgo_sb[:, CHUNK * c : CHUNK * (c + 1)],
+                MULT,
+            )
+
+        def finish(q):
+            for half in range(2):
+                cols = slice(512 * half, 512 * (half + 1))
+                res = ring.tile([P, 512], F32, name="res", bufs=4)
+                nc.vector.scalar_tensor_tensor(res[:], pages[q][:, cols], 1.0, x0_sb[q][:, cols], ADD, MULT)
+                nc.sync.dma_start(out=out[P * q : P * (q + 1), cols], in_=res[:])
+
+        h00 = make_h(0, 0)
+        gather_words(1, 1)
+        quantise_h(0, 0, h00)
+        h01 = make_h(0, 1)
+        quantise_w1(0, 1)
+        quantise_h(0, 1, h01)
+        h02 = make_h(0, 2)
+        quantise_w1(1, 1)
+        quantise_h(0, 2, h02)
+        h10 = make_h(1, 0)
+        quantise_h(1, 0, h10)
+        y0 = make_y(0)
+        h11 = make_h(1, 1)
+        scatter(0, 0, y0)
+        quantise_h(1, 1, h11)
+        y1 = make_y(1)
+        for q in range(1, 4):
+            scatter(0, q, y0)
+        h12 = make_h(1, 2)
+        scatter(1, 0, y1)
+        quantise_h(1, 2, h12)
+        y2 = make_y(2)
+        for q in range(1, 4):
+            scatter(1, q, y1)
+        h03 = make_h(0, 3)
+        h13 = make_h(1, 3)
+        quantise_h(0, 3, h03)
+        scatter(2, 0, y2)
+        quantise_h(1, 3, h13)
+        y3 = make_y(3)
+        for q in range(1, 4):
+            scatter(2, q, y2)
+        scatter(3, 0, y3)
+        for q in range(1, 4):
+            scatter(3, q, y3)
+            finish(q - 1)
+        finish(3)

@@ -41,18 +41,22 @@ def tile_list_kidney_mesh_stress_kernel(
 
         tab_sc = keep.tile([P, T], U8, name="tab_sc", align_bytes=64)
         w4_sc = keep.tile([P, 2, N], U8, name="w4_sc", align_bytes=64)
-        nc.gpsimd.memset(tab_sc[:].bitcast(I32), 0)
-        for q in range(4):
-            nc.gpsimd.dma_start(
-                out=tab_sc[32 * q : 32 * q + 8, :].bitcast(I32),
-                in_=tab_scales[:, 4 * q : 4 * q + 4, :].bitcast(I32),
-            )
-        nc.gpsimd.memset(w4_sc[:].rearrange("p a n -> p (a n)").bitcast(I32), 0)
-        for q in range(4):
-            nc.gpsimd.dma_start(
-                out=w4_sc[32 * q : 32 * q + 4, :, :].bitcast(I32),
-                in_=w4_scales[:, 4 * q : 4 * q + 4, :].rearrange("a r n -> r a n").bitcast(I32),
-            )
+        nc.vector.memset(tab_sc[:].bitcast(I32), 0)
+        nc.vector.memset(w4_sc[:].rearrange("p a n -> p (a n)").bitcast(I32), 0)
+
+        def load_tab_scales():
+            for q in range(4):
+                nc.sync.dma_start(
+                    out=tab_sc[32 * q : 32 * q + 8, :].bitcast(I32),
+                    in_=tab_scales[:, 4 * q : 4 * q + 4, :].bitcast(I32),
+                )
+
+        def load_w4_scales():
+            for q in range(4):
+                nc.sync.dma_start(
+                    out=w4_sc[32 * q : 32 * q + 4, :, :].bitcast(I32),
+                    in_=w4_scales[:, 4 * q : 4 * q + 4, :].rearrange("a r n -> r a n").bitcast(I32),
+                )
 
         w1_raw = {}
         w1_codes = {}
@@ -79,7 +83,7 @@ def tile_list_kidney_mesh_stress_kernel(
             tab_sb[a] = words
 
         def load_stiff(b, c):
-            st = keep.tile([P, PACK, CHUNK], F32, name=f"stiff{b}{c}")
+            st = ring.tile([P, PACK, CHUNK], F32, name="stiff_raw", bufs=6)
             nc.sync.dma_start(
                 out=st[:],
                 in_=stiff[KP * b : KP * (b + 1), CHUNK * c : CHUNK * (c + 1)].rearrange("(p t) j -> p t j", t=PACK),
@@ -88,6 +92,7 @@ def tile_list_kidney_mesh_stress_kernel(
 
         nc.sync.dma_start(offs_sb[:], offs)
         load_w1(0, 0)
+        load_tab_scales()
         load_w1(1, 0)
         load_tab(0)
         load_tab(1)
@@ -96,15 +101,16 @@ def tile_list_kidney_mesh_stress_kernel(
         load_w1(0, 1)
         load_stiff(0, 2)
         load_w1(1, 1)
+        load_stiff(0, 3)
         load_stiff(1, 0)
         w4_sb = keep.tile([P, 2, 2 * N], U8, name="w4_sb", align_bytes=64)
         nc.sync.dma_start(out=w4_sb[:].bitcast(I32), in_=w4_words.rearrange("a p n -> p a n").bitcast(I32))
+        load_stiff(1, 1)
+        load_w4_scales()
         nc.sync.dma_start(offs2_sb[:], offs2)
         wgo_sb = keep.tile([P, S], F32, name="wgo_sb")
         nc.sync.dma_start(out=wgo_sb[:], in_=wgo)
-        load_stiff(1, 1)
         load_stiff(1, 2)
-        load_stiff(0, 3)
         load_stiff(1, 3)
         x0_sb = []
         for q in range(4):
@@ -115,8 +121,8 @@ def tile_list_kidney_mesh_stress_kernel(
         def quantise_w1(a, b):
             grouped = ring.tile([P, KP * PACK], BF16, name="w1_bf", align_bytes=64, bufs=2)
             nc.scalar.copy(
-                out=grouped[:].rearrange("p (th tl m j) -> p th m j tl", th=2, tl=2, j=PACK),
-                in_=w1_raw[a, b][:].rearrange("p j (m th tl) -> p th m j tl", th=2, tl=2),
+                out=grouped[:].rearrange("p (t m j) -> p m t j", t=PACK, j=PACK),
+                in_=w1_raw[a, b][:].rearrange("p j (m t) -> p m t j", t=PACK),
             )
             codes = keep.tile([P, KP], U32, name=f"w1_codes{a}{b}", align_bytes=64)
             sc = keep.tile([P, KP], U8, name=f"w1_sc{a}{b}", align_bytes=64)
@@ -158,19 +164,19 @@ def tile_list_kidney_mesh_stress_kernel(
                             start=(a == 0),
                             stop=(a == 1),
                         )
-                u = ring.tile([P, BANK_J * PACK], F32, name="u", bufs=4)
-                nc.vector.tensor_tensor(
-                    u[:].rearrange("p (c i t) -> p c t i", i=2, t=PACK),
-                    bank[:].rearrange("p t (c i) -> p c t i", i=2),
-                    stiff_sb[b, c][:, :, BANK_J * s : BANK_J * (s + 1)].rearrange("p t (c i) -> p c t i", i=2),
-                    MULT,
+                woven = ring.tile([P, BANK_J, PACK], F32, name="stiff_woven", bufs=6)
+                nc.scalar.copy(
+                    out=woven[:],
+                    in_=stiff_sb[b, c][:, :, BANK_J * s : BANK_J * (s + 1)].rearrange("p t j -> p j t"),
                 )
+                u = ring.tile([P, BANK_J, PACK], F32, name="u", bufs=4)
+                nc.vector.tensor_tensor(u[:], bank[:].rearrange("p t j -> p j t"), woven[:], MULT)
                 banks.append(bank)
                 us.append(u)
             for s in range(CHUNK // BANK_J):
                 nc.vector.scalar_tensor_tensor(
                     h_bf[:, BANK_J * PACK * s : BANK_J * PACK * (s + 1)].rearrange("p (j t) -> p j t", t=PACK),
-                    us[s][:].rearrange("p (j t) -> p j t", t=PACK),
+                    us[s][:],
                     1.0,
                     banks[s][:].rearrange("p t j -> p j t"),
                     ADD,
@@ -230,35 +236,25 @@ def tile_list_kidney_mesh_stress_kernel(
         quantise_h(0, 0, h00)
         h01 = make_h(0, 1)
         quantise_w1(0, 1)
-        quantise_h(0, 1, h01)
         h02 = make_h(0, 2)
+        quantise_h(0, 1, h01)
         quantise_w1(1, 1)
+        h03 = make_h(0, 3)
         quantise_h(0, 2, h02)
         h10 = make_h(1, 0)
-        quantise_h(1, 0, h10)
-        y0 = make_y(0)
-        h11 = make_h(1, 1)
-        scatter(0, 0, y0)
-        quantise_h(1, 1, h11)
-        y1 = make_y(1)
-        for q in range(1, 4):
-            scatter(0, q, y0)
-        h12 = make_h(1, 2)
-        scatter(1, 0, y1)
-        quantise_h(1, 2, h12)
-        y2 = make_y(2)
-        for q in range(1, 4):
-            scatter(1, q, y1)
-        h03 = make_h(0, 3)
-        h13 = make_h(1, 3)
         quantise_h(0, 3, h03)
-        scatter(2, 0, y2)
-        quantise_h(1, 3, h13)
-        y3 = make_y(3)
+        quantise_h(1, 0, h10)
+        ys = make_y(0)
+        for c in range(1, 4):
+            h1c = make_h(1, c)
+            scatter(c - 1, 0, ys)
+            quantise_h(1, c, h1c)
+            ys_next = make_y(c)
+            for q in range(1, 4):
+                scatter(c - 1, q, ys)
+            ys = ys_next
+        scatter(3, 0, ys)
         for q in range(1, 4):
-            scatter(2, q, y2)
-        scatter(3, 0, y3)
-        for q in range(1, 4):
-            scatter(3, q, y3)
+            scatter(3, q, ys)
             finish(q - 1)
         finish(3)

@@ -16,25 +16,27 @@ FP4X4 = mybir.dt.float4_e2m1fn_x4
 MULT = mybir.AluOpType.mult
 ADD = mybir.AluOpType.add
 COPY = mybir.ActivationFunctionType.Copy
+SQUARE = mybir.ActivationFunctionType.Square
 
 P = 128
 PACK = 4
 KP = P * PACK
-CHUNK = 256
-BANK_J = 128
+BANK = 512
+BANK_J = BANK // PACK
+GROUPS = [(0, 256), (256, 256), (512, 512)]
 
 
 def tile_list_kidney_mesh_stress_kernel(
     tc, tab_words, tab_scales, offs, w1, stiff, w4_words, w4_scales, offs2, wgo, x0, out
 ):
     nc = tc.nc
-    n_chunks = S // CHUNK
 
     with ExitStack() as ctx:
         keep = ctx.enter_context(tc.tile_pool(name="keep", bufs=1))
         ring = ctx.enter_context(tc.tile_pool(name="ring", bufs=3))
-        psum_d = ctx.enter_context(tc.psum_pool(name="psum_d", bufs=5))
-        psum_y = ctx.enter_context(tc.psum_pool(name="psum_y", bufs=3))
+        shared = ctx.enter_context(tc.tile_pool(name="shared", bufs=1))
+        psum_d = ctx.enter_context(tc.psum_pool(name="psum_d", bufs=6))
+        psum_y = ctx.enter_context(tc.psum_pool(name="psum_y", bufs=2))
 
         offs_sb = keep.tile([P, S // 16], U16, name="offs_sb")
         offs2_sb = keep.tile([P, S // 16], U16, name="offs2_sb")
@@ -44,114 +46,98 @@ def tile_list_kidney_mesh_stress_kernel(
         nc.vector.memset(tab_sc[:].bitcast(I32), 0)
         nc.vector.memset(w4_sc[:].rearrange("p a n -> p (a n)").bitcast(I32), 0)
 
-        def load_tab_scales():
-            for q in range(4):
-                nc.sync.dma_start(
-                    out=tab_sc[32 * q : 32 * q + 8, :].bitcast(I32),
-                    in_=tab_scales[:, 4 * q : 4 * q + 4, :].bitcast(I32),
-                )
-
-        def load_w4_scales():
-            for q in range(4):
-                nc.sync.dma_start(
-                    out=w4_sc[32 * q : 32 * q + 4, :, :].bitcast(I32),
-                    in_=w4_scales[:, 4 * q : 4 * q + 4, :].rearrange("a r n -> r a n").bitcast(I32),
-                )
-
         w1_raw = {}
-        w1_codes = {}
-        w1_sc = {}
-        stiff_sb = {}
         tab_sb = {}
-        h_codes = {}
-        h_sc = {}
+        stiff_sb = {}
 
-        def load_w1(a, b):
-            raw = keep.tile([P, PACK, KP], F32, name=f"w1_raw{a}{b}")
-            nc.sync.dma_start(
-                out=raw[:],
-                in_=w1[KP * a : KP * (a + 1), KP * b : KP * (b + 1)].rearrange("(p j) c -> p j c", j=PACK),
-            )
-            w1_raw[a, b] = raw
+        def load_w1(a):
+            w1_raw[a] = keep.tile([P, PACK, H], F32, name=f"w1_raw{a}")
+            nc.sync.dma_start(out=w1_raw[a][:], in_=w1[KP * a : KP * (a + 1), :].rearrange("(p j) c -> p j c", j=PACK))
 
         def load_tab(a):
-            words = keep.tile([P, T], U32, name=f"tab{a}")
+            tab_sb[a] = keep.tile([P, T], U32, name=f"tab{a}")
             nc.sync.dma_start(
-                out=words[:].bitcast(I32),
+                out=tab_sb[a][:].bitcast(I32),
                 in_=tab_words[a].rearrange("p n t -> p (n t)").bitcast(I32),
             )
-            tab_sb[a] = words
 
-        def load_stiff(b, c):
-            st = ring.tile([P, PACK, CHUNK], F32, name="stiff_raw", bufs=6)
+        def load_stiff(b, g):
+            j0, width = GROUPS[g]
+            stiff_sb[b, g] = keep.tile([P, PACK, width], F32, name=f"stiff{b}{g}")
             nc.sync.dma_start(
-                out=st[:],
-                in_=stiff[KP * b : KP * (b + 1), CHUNK * c : CHUNK * (c + 1)].rearrange("(p t) j -> p t j", t=PACK),
+                out=stiff_sb[b, g][:],
+                in_=stiff[KP * b : KP * (b + 1), j0 : j0 + width].rearrange("(p t) j -> p t j", t=PACK),
             )
-            stiff_sb[b, c] = st
 
         nc.sync.dma_start(offs_sb[:], offs)
-        load_w1(0, 0)
-        load_tab_scales()
-        load_w1(1, 0)
+        load_w1(0)
+        for q in range(4):
+            nc.sync.dma_start(
+                out=tab_sc[32 * q : 32 * q + 8, :].bitcast(I32),
+                in_=tab_scales[:, 4 * q : 4 * q + 4, :].bitcast(I32),
+            )
+        load_w1(1)
         load_tab(0)
         load_tab(1)
         load_stiff(0, 0)
-        load_stiff(0, 1)
-        load_w1(0, 1)
-        load_stiff(0, 2)
-        load_w1(1, 1)
-        load_stiff(0, 3)
         load_stiff(1, 0)
+        load_stiff(0, 1)
+        load_stiff(1, 1)
         w4_sb = keep.tile([P, 2, 2 * N], U8, name="w4_sb", align_bytes=64)
         nc.sync.dma_start(out=w4_sb[:].bitcast(I32), in_=w4_words.rearrange("a p n -> p a n").bitcast(I32))
-        load_stiff(1, 1)
-        load_w4_scales()
-        nc.sync.dma_start(offs2_sb[:], offs2)
+        for q in range(4):
+            nc.sync.dma_start(
+                out=w4_sc[32 * q : 32 * q + 4, :, :].bitcast(I32),
+                in_=w4_scales[:, 4 * q : 4 * q + 4, :].rearrange("a r n -> r a n").bitcast(I32),
+            )
         wgo_sb = keep.tile([P, S], F32, name="wgo_sb")
         nc.sync.dma_start(out=wgo_sb[:], in_=wgo)
+        nc.sync.dma_start(offs2_sb[:], offs2)
+        load_stiff(0, 2)
         load_stiff(1, 2)
-        load_stiff(1, 3)
-        x0_sb = []
-        for q in range(4):
-            xt = keep.tile([P, S], F32, name=f"x0_{q}")
-            nc.sync.dma_start(out=xt[:], in_=x0[P * q : P * (q + 1), :])
-            x0_sb.append(xt)
+
+        w1_codes = {}
+        w1_sc = {}
 
         def quantise_w1(a, b):
-            grouped = ring.tile([P, KP * PACK], BF16, name="w1_bf", align_bytes=64, bufs=2)
-            nc.scalar.copy(
-                out=grouped[:].rearrange("p (t m j) -> p m t j", t=PACK, j=PACK),
-                in_=w1_raw[a, b][:].rearrange("p j (m t) -> p m t j", t=PACK),
-            )
-            codes = keep.tile([P, KP], U32, name=f"w1_codes{a}{b}", align_bytes=64)
-            sc = keep.tile([P, KP], U8, name=f"w1_sc{a}{b}", align_bytes=64)
-            nc.vector.quantize_mx(out=codes[:].bitcast(FP8X4), scales=sc[:], in_=grouped[:])
-            w1_codes[a, b] = codes
-            w1_sc[a, b] = sc
+            grouped = ring.tile([P, KP * PACK], BF16, name="w1_bf", align_bytes=64)
+            dst = grouped[:].rearrange("p (t m j) -> p m t j", t=PACK, j=PACK)
+            src = w1_raw[a][:, :, KP * b : KP * (b + 1)].rearrange("p j (m t) -> p m t j", t=PACK)
+            if a == 0:
+                nc.scalar.copy(out=dst, in_=src)
+            else:
+                nc.vector.tensor_copy(out=dst, in_=src)
+            w1_codes[a, b] = keep.tile([P, KP], U32, name=f"w1_codes{a}{b}", align_bytes=64)
+            w1_sc[a, b] = keep.tile([P, KP], U8, name=f"w1_sc{a}{b}", align_bytes=64)
+            nc.vector.quantize_mx(out=w1_codes[a, b][:].bitcast(FP8X4), scales=w1_sc[a, b][:], in_=grouped[:])
 
         v_words = {}
 
         def gather_words(a, half):
-            picked = keep.tile([P, S // 2], U32, name=f"v_words{a}{half}", align_bytes=64)
-            nc.vector.tensor_copy(picked[:], tab_sb[a][:].indirect(offs_sb[:, 32 * half : 32 * (half + 1)]))
-            v_words[a, half] = picked
+            v_words[a, half] = keep.tile([P, S // 2], U32, name=f"v_words{a}{half}", align_bytes=64)
+            nc.vector.tensor_copy(v_words[a, half][:], tab_sb[a][:].indirect(offs_sb[:, 32 * half : 32 * (half + 1)]))
 
-        quantise_w1(0, 0)
         v_sc = keep.tile([P, S], U8, name="v_sc", align_bytes=64)
         nc.vector.tensor_copy(v_sc[:], tab_sc[:].indirect(offs_sb[:]))
-        quantise_w1(1, 0)
-        gather_words(0, 0)
-        gather_words(0, 1)
-        gather_words(1, 0)
+        for a in range(2):
+            for b in range(2):
+                quantise_w1(a, b)
+        x0_sb = w1_raw[0]
+        for q in range(4):
+            nc.sync.dma_start(out=x0_sb[:, q, :], in_=x0[P * q : P * (q + 1), :])
+        for a in range(2):
+            for half in range(2):
+                gather_words(a, half)
 
-        def make_h(b, c):
-            h_bf = ring.tile([P, CHUNK * PACK], BF16, name="h_bf", align_bytes=64)
+        h_codes = {}
+        h_sc = {}
+
+        def make_h(b, g, vector_banks, h_bf):
+            j0, width = GROUPS[g]
             banks = []
-            us = []
-            for s in range(CHUNK // BANK_J):
-                j0 = CHUNK * c + BANK_J * s
-                half, jh = divmod(j0, S // 2)
+            mids = []
+            for lo in range(0, width, BANK_J):
+                half, jh = divmod(j0 + lo, S // 2)
                 bank = psum_d.tile([P, PACK, BANK_J], F32, name="d_bank")
                 for t in range(PACK):
                     for a in range(2):
@@ -160,101 +146,140 @@ def tile_list_kidney_mesh_stress_kernel(
                             lhsT=w1_codes[a, b][:, P * t : P * (t + 1)].bitcast(FP8X4),
                             lhsT_scale=w1_sc[a, b][:, P * t : P * (t + 1)],
                             rhs=v_words[a, half][:, jh : jh + BANK_J].bitcast(FP8X4),
-                            rhs_scale=v_sc[4 * a :, j0 : j0 + BANK_J],
+                            rhs_scale=v_sc[4 * a :, j0 + lo : j0 + lo + BANK_J],
                             start=(a == 0),
                             stop=(a == 1),
                         )
-                woven = ring.tile([P, BANK_J, PACK], F32, name="stiff_woven", bufs=6)
-                nc.scalar.copy(
-                    out=woven[:],
-                    in_=stiff_sb[b, c][:, :, BANK_J * s : BANK_J * (s + 1)].rearrange("p t j -> p j t"),
-                )
-                u = ring.tile([P, BANK_J, PACK], F32, name="u", bufs=4)
-                nc.vector.tensor_tensor(u[:], bank[:].rearrange("p t j -> p j t"), woven[:], MULT)
+                stiff_rows = stiff_sb[b, g][:, :, lo : lo + BANK_J]
+                mid = ring.tile([P, BANK], F32, name="mid", bufs=6)
+                if lo < BANK_J * vector_banks:
+                    woven = ring.tile([P, BANK_J, PACK], F32, name="stiff_woven")
+                    nc.scalar.copy(out=woven[:], in_=stiff_rows.rearrange("p t j -> p j t"))
+                    nc.vector.tensor_tensor(
+                        mid[:].rearrange("p (j t) -> p j t", t=PACK),
+                        bank[:].rearrange("p t j -> p j t"),
+                        woven[:],
+                        MULT,
+                    )
+                else:
+                    sq = ring.tile([P, BANK_J // 2, PACK, 2], F32, name="sq")
+                    nc.scalar.activation(sq[:], bank[:].rearrange("p t (c i) -> p c t i", i=2), SQUARE)
+                    nc.gpsimd.tensor_tensor(
+                        mid[:].rearrange("p (c t i) -> p c t i", t=PACK, i=2),
+                        sq[:],
+                        stiff_rows.rearrange("p t (c i) -> p c t i", i=2),
+                        MULT,
+                    )
                 banks.append(bank)
-                us.append(u)
-            for s in range(CHUNK // BANK_J):
-                nc.vector.scalar_tensor_tensor(
-                    h_bf[:, BANK_J * PACK * s : BANK_J * PACK * (s + 1)].rearrange("p (j t) -> p j t", t=PACK),
-                    us[s][:],
-                    1.0,
-                    banks[s][:].rearrange("p t j -> p j t"),
-                    ADD,
-                    MULT,
-                )
-            return h_bf
+                mids.append(mid)
+            for s in range(width // BANK_J):
+                h_part = h_bf[:, BANK * s : BANK * (s + 1)]
+                if s < vector_banks:
+                    nc.vector.scalar_tensor_tensor(
+                        h_part.rearrange("p (j t) -> p j t", t=PACK),
+                        mids[s][:].rearrange("p (j t) -> p j t", t=PACK),
+                        1.0,
+                        banks[s][:].rearrange("p t j -> p j t"),
+                        ADD,
+                        MULT,
+                    )
+                else:
+                    nc.vector.tensor_tensor(
+                        h_part.rearrange("p (c i t) -> p c i t", i=2, t=PACK),
+                        banks[s][:].rearrange("p t (c i) -> p c i t", i=2),
+                        mids[s][:].rearrange("p (c t i) -> p c i t", t=PACK, i=2),
+                        ADD,
+                    )
 
-        def quantise_h(b, c, h_bf):
-            codes = keep.tile([P, CHUNK], U32, name=f"h_codes{b}{c}", align_bytes=64)
-            sc = keep.tile([P, CHUNK], U8, name=f"h_sc{b}{c}", align_bytes=64)
-            nc.vector.quantize_mx(out=codes[:].bitcast(FP8X4), scales=sc[:], in_=h_bf[:])
-            h_codes[b, c] = codes
-            h_sc[b, c] = sc
+        def quantise_h(b, g, h_bf):
+            width = GROUPS[g][1]
+            h_codes[b, g] = keep.tile([P, width], U32, name=f"h_codes{b}{g}", align_bytes=64)
+            h_sc[b, g] = keep.tile([P, width], U8, name=f"h_sc{b}{g}", align_bytes=64)
+            nc.vector.quantize_mx(out=h_codes[b, g][:].bitcast(FP8X4), scales=h_sc[b, g][:], in_=h_bf[:])
 
-        pages = [keep.tile([P, S], F32, name=f"page{q}") for q in range(4)]
-
-        def make_y(c):
+        def make_y(g):
+            width = GROUPS[g][1]
+            per_bank = BANK // width
+            step = BANK if width == BANK else BANK_J
             ys = []
-            for pair in range(2):
-                bank = psum_y.tile([P, 2, CHUNK], F32, name="y_bank")
-                for qq in range(2):
-                    q = 2 * pair + qq
-                    for s in range(CHUNK // BANK_J):
-                        cols = slice(BANK_J * s, BANK_J * (s + 1))
+            for first in range(0, 4, per_bank):
+                bank = psum_y.tile([P, per_bank, width], F32, name="y_bank")
+                for qq in range(per_bank):
+                    q = first + qq
+                    for lo in range(0, width, step):
+                        cols = slice(lo, lo + step)
                         for b in range(2):
                             nc.tensor.matmul_mx(
                                 out=bank[:, qq, cols],
                                 lhsT=w4_sb[:, b, 2 * P * q : 2 * P * (q + 1)].bitcast(FP4X4),
                                 lhsT_scale=w4_sc[:, b, P * q : P * (q + 1)],
-                                rhs=h_codes[b, c][:, cols].bitcast(FP8X4),
-                                rhs_scale=h_sc[b, c][:, cols],
+                                rhs=h_codes[b, g][:, cols].bitcast(FP8X4),
+                                rhs_scale=h_sc[b, g][:, cols],
                                 start=(b == 0),
                                 stop=(b == 1),
                             )
-                y_neg = ring.tile([P, 2, CHUNK], F32, name="y_neg", bufs=4)
+                y_neg = ring.tile([P, per_bank, width], F32, name="y_neg", bufs=4)
                 nc.scalar.activation(y_neg[:], bank[:], COPY, scale=-1.0)
-                ys.append(y_neg)
+                ys.extend([y_neg[:, qq, :] for qq in range(per_bank)])
             return ys
 
-        def scatter(c, q, ys):
-            nc.vector.tensor_tensor(
-                pages[q][:].indirect(offs2_sb[:, 16 * c : 16 * (c + 1)]),
-                ys[q // 2][:, q % 2, :],
-                wgo_sb[:, CHUNK * c : CHUNK * (c + 1)],
-                MULT,
+        z_sb = [keep.tile([P, S], F32, name=f"z{q}") for q in range(4)]
+
+        def make_z(g, ys):
+            j0, width = GROUPS[g]
+            for q in range(4):
+                nc.gpsimd.tensor_tensor(z_sb[q][:, j0 : j0 + width], ys[q], wgo_sb[:, j0 : j0 + width], MULT)
+
+        pages = {q: keep.tile([P, S], F32, name=f"page{q}") for q in range(3)}
+
+        def scatter(q, j0, width):
+            nc.vector.tensor_copy(
+                pages[q][:].indirect(offs2_sb[:, j0 // 16 : (j0 + width) // 16]), z_sb[q][:, j0 : j0 + width]
             )
 
-        def finish(q):
+        def finish(q, on_vector):
             for half in range(2):
-                cols = slice(512 * half, 512 * (half + 1))
-                res = ring.tile([P, 512], F32, name="res", bufs=4)
-                nc.vector.scalar_tensor_tensor(res[:], pages[q][:, cols], 1.0, x0_sb[q][:, cols], ADD, MULT)
-                nc.sync.dma_start(out=out[P * q : P * (q + 1), cols], in_=res[:])
+                cols = slice(BANK * half, BANK * (half + 1))
+                res = ring.tile([P, BANK], F32, name="res")
+                if on_vector:
+                    nc.vector.scalar_tensor_tensor(res[:], pages[q][:, cols], 1.0, x0_sb[:, q, cols], ADD, MULT)
+                else:
+                    factor = ring.tile([P, BANK], F32, name="factor", bufs=2)
+                    nc.scalar.activation(factor[:], pages[q][:, cols], COPY, bias=1.0)
+                    nc.gpsimd.tensor_tensor(res[:], factor[:], x0_sb[:, q, cols], MULT)
+                queue = nc.scalar if on_vector else nc.sync
+                queue.dma_start(out=out[P * q : P * (q + 1), cols], in_=res[:])
 
-        h00 = make_h(0, 0)
-        gather_words(1, 1)
-        quantise_h(0, 0, h00)
-        h01 = make_h(0, 1)
-        quantise_w1(0, 1)
-        h02 = make_h(0, 2)
-        quantise_h(0, 1, h01)
-        quantise_w1(1, 1)
-        h03 = make_h(0, 3)
-        quantise_h(0, 2, h02)
-        h10 = make_h(1, 0)
-        quantise_h(0, 3, h03)
-        quantise_h(1, 0, h10)
-        ys = make_y(0)
-        for c in range(1, 4):
-            h1c = make_h(1, c)
-            scatter(c - 1, 0, ys)
-            quantise_h(1, c, h1c)
-            ys_next = make_y(c)
-            for q in range(1, 4):
-                scatter(c - 1, q, ys)
-            ys = ys_next
-        scatter(3, 0, ys)
-        for q in range(1, 4):
-            scatter(3, q, ys)
-            finish(q - 1)
-        finish(3)
+        h_bf = {}
+        for b in range(2):
+            for g in range(2):
+                h_bf[b, g] = keep.tile([P, PACK * GROUPS[g][1]], BF16, name=f"h_bf{b}{g}", align_bytes=64)
+        h_bf[0, 2] = keep.tile([P, PACK * GROUPS[2][1]], BF16, name="h_bf02", align_bytes=64)
+        h_bf[1, 2] = shared.tile([P, PACK * GROUPS[2][1]], BF16, name="h_bf12", align_bytes=64, offset=0)
+
+        make_h(0, 0, 2, h_bf[0, 0])
+        make_h(1, 0, 2, h_bf[1, 0])
+        quantise_h(0, 0, h_bf[0, 0])
+        quantise_h(1, 0, h_bf[1, 0])
+        y0 = make_y(0)
+        make_h(0, 1, 2, h_bf[0, 1])
+        make_h(1, 1, 0, h_bf[1, 1])
+        quantise_h(0, 1, h_bf[0, 1])
+        quantise_h(1, 1, h_bf[1, 1])
+        make_z(0, y0)
+        y1 = make_y(1)
+        for q in range(3):
+            scatter(q, 0, 256)
+        make_h(0, 2, 0, h_bf[0, 2])
+        quantise_h(0, 2, h_bf[0, 2])
+        make_z(1, y1)
+        for q in range(3):
+            scatter(q, 256, 256)
+        make_h(1, 2, 0, h_bf[1, 2])
+        quantise_h(1, 2, h_bf[1, 2])
+        pages[3] = shared.tile([P, S], F32, name="page3", align_bytes=64, offset=0)
+        scatter(3, 0, 512)
+        make_z(2, make_y(2))
+        for q in range(4):
+            scatter(q, 512, 512)
+            finish(q, q == 3)

@@ -21,9 +21,14 @@ SQUARE = mybir.ActivationFunctionType.Square
 P = 128
 PACK = 4
 KP = P * PACK
+PASSES = K // KP
+N_TILES = N // P
 BANK = 512
 BANK_J = BANK // PACK
+PER_COL = 16
+HALF = S // 2
 GROUPS = [(0, 256), (256, 256), (512, 512)]
+VECTOR_PIECES = [(0, 0), (1, 0), (0, 1)]
 
 
 def tile_list_kidney_mesh_stress_kernel(
@@ -38,11 +43,11 @@ def tile_list_kidney_mesh_stress_kernel(
         psum_d = ctx.enter_context(tc.psum_pool(name="psum_d", bufs=6))
         psum_y = ctx.enter_context(tc.psum_pool(name="psum_y", bufs=2))
 
-        offs_sb = keep.tile([P, S // 16], U16, name="offs_sb")
-        offs2_sb = keep.tile([P, S // 16], U16, name="offs2_sb")
+        offs_sb = keep.tile([P, S // PER_COL], U16, name="offs_sb")
+        offs2_sb = keep.tile([P, S // PER_COL], U16, name="offs2_sb")
 
         tab_sc = keep.tile([P, T], U8, name="tab_sc", align_bytes=64)
-        w4_sc = keep.tile([P, 2, N], U8, name="w4_sc", align_bytes=64)
+        w4_sc = keep.tile([P, PASSES, N], U8, name="w4_sc", align_bytes=64)
         nc.vector.memset(tab_sc[:].bitcast(I32), 0)
         nc.vector.memset(w4_sc[:].rearrange("p a n -> p (a n)").bitcast(I32), 0)
 
@@ -73,17 +78,16 @@ def tile_list_kidney_mesh_stress_kernel(
         load_w1(0)
         for q in range(4):
             nc.sync.dma_start(
-                out=tab_sc[32 * q : 32 * q + 8, :].bitcast(I32),
+                out=tab_sc[32 * q : 32 * q + 4 * PASSES, :].bitcast(I32),
                 in_=tab_scales[:, 4 * q : 4 * q + 4, :].bitcast(I32),
             )
         load_w1(1)
         load_tab(0)
         load_tab(1)
-        load_stiff(0, 0)
-        load_stiff(1, 0)
-        load_stiff(0, 1)
-        load_stiff(1, 1)
-        w4_sb = keep.tile([P, 2, 2 * N], U8, name="w4_sb", align_bytes=64)
+        for g in range(2):
+            for b in range(PASSES):
+                load_stiff(b, g)
+        w4_sb = keep.tile([P, PASSES, 2 * N], U8, name="w4_sb", align_bytes=64)
         nc.sync.dma_start(out=w4_sb[:].bitcast(I32), in_=w4_words.rearrange("a p n -> p a n").bitcast(I32))
         for q in range(4):
             nc.sync.dma_start(
@@ -93,8 +97,8 @@ def tile_list_kidney_mesh_stress_kernel(
         wgo_sb = keep.tile([P, S], F32, name="wgo_sb")
         nc.sync.dma_start(out=wgo_sb[:], in_=wgo)
         nc.sync.dma_start(offs2_sb[:], offs2)
-        load_stiff(0, 2)
-        load_stiff(1, 2)
+        for b in range(PASSES):
+            load_stiff(b, 2)
 
         w1_codes = {}
         w1_sc = {}
@@ -103,44 +107,46 @@ def tile_list_kidney_mesh_stress_kernel(
             grouped = ring.tile([P, KP * PACK], BF16, name="w1_bf", align_bytes=64)
             dst = grouped[:].rearrange("p (t m j) -> p m t j", t=PACK, j=PACK)
             src = w1_raw[a][:, :, KP * b : KP * (b + 1)].rearrange("p j (m t) -> p m t j", t=PACK)
-            if a == 0:
-                nc.scalar.copy(out=dst, in_=src)
-            else:
+            if (a, b) == (1, 0):
                 nc.vector.tensor_copy(out=dst, in_=src)
+            else:
+                nc.scalar.copy(out=dst, in_=src)
             w1_codes[a, b] = keep.tile([P, KP], U32, name=f"w1_codes{a}{b}", align_bytes=64)
             w1_sc[a, b] = keep.tile([P, KP], U8, name=f"w1_sc{a}{b}", align_bytes=64)
             nc.vector.quantize_mx(out=w1_codes[a, b][:].bitcast(FP8X4), scales=w1_sc[a, b][:], in_=grouped[:])
 
-        v_words = {}
-
-        def gather_words(a, half):
-            v_words[a, half] = keep.tile([P, S // 2], U32, name=f"v_words{a}{half}", align_bytes=64)
-            nc.vector.tensor_copy(v_words[a, half][:], tab_sb[a][:].indirect(offs_sb[:, 32 * half : 32 * (half + 1)]))
-
         v_sc = keep.tile([P, S], U8, name="v_sc", align_bytes=64)
         nc.vector.tensor_copy(v_sc[:], tab_sc[:].indirect(offs_sb[:]))
-        for a in range(2):
-            for b in range(2):
+        for a in range(PASSES):
+            for b in range(PASSES):
                 quantise_w1(a, b)
-        x0_sb = w1_raw[0]
-        for q in range(4):
-            nc.sync.dma_start(out=x0_sb[:, q, :], in_=x0[P * q : P * (q + 1), :])
-        for a in range(2):
-            for half in range(2):
-                gather_words(a, half)
 
+        x0_sb = w1_raw[0]
+        for q in range(N_TILES):
+            nc.sync.dma_start(out=x0_sb[:, q, :], in_=x0[P * q : P * (q + 1), :])
+
+        v_words = {}
+        for a in range(PASSES):
+            for half in range(2):
+                v_words[a, half] = keep.tile([P, HALF], U32, name=f"v_words{a}{half}", align_bytes=64)
+                entries = offs_sb[:, HALF * half // PER_COL : HALF * (half + 1) // PER_COL]
+                nc.vector.tensor_copy(v_words[a, half][:], tab_sb[a][:].indirect(entries))
+
+        h_bf = {}
         h_codes = {}
         h_sc = {}
 
-        def make_h(b, g, vector_banks, h_bf):
+        def make_h(b, g, pool, **place):
             j0, width = GROUPS[g]
-            banks = []
-            mids = []
-            for lo in range(0, width, BANK_J):
-                half, jh = divmod(j0 + lo, S // 2)
+            on_vector = (b, g) in VECTOR_PIECES
+            h_bf[b, g] = pool.tile([P, PACK * width], BF16, name=f"h_bf{b}{g}", align_bytes=64, **place)
+            pending = []
+            for s in range(width // BANK_J):
+                lo = BANK_J * s
+                half, jh = divmod(j0 + lo, HALF)
                 bank = psum_d.tile([P, PACK, BANK_J], F32, name="d_bank")
                 for t in range(PACK):
-                    for a in range(2):
+                    for a in range(PASSES):
                         nc.tensor.matmul_mx(
                             out=bank[:, t, :],
                             lhsT=w1_codes[a, b][:, P * t : P * (t + 1)].bitcast(FP8X4),
@@ -148,138 +154,108 @@ def tile_list_kidney_mesh_stress_kernel(
                             rhs=v_words[a, half][:, jh : jh + BANK_J].bitcast(FP8X4),
                             rhs_scale=v_sc[4 * a :, j0 + lo : j0 + lo + BANK_J],
                             start=(a == 0),
-                            stop=(a == 1),
+                            stop=(a == PASSES - 1),
                         )
-                stiff_rows = stiff_sb[b, g][:, :, lo : lo + BANK_J]
-                mid = ring.tile([P, BANK], F32, name="mid", bufs=6)
-                if lo < BANK_J * vector_banks:
-                    woven = ring.tile([P, BANK_J, PACK], F32, name="stiff_woven")
-                    nc.scalar.copy(out=woven[:], in_=stiff_rows.rearrange("p t j -> p j t"))
-                    nc.vector.tensor_tensor(
-                        mid[:].rearrange("p (j t) -> p j t", t=PACK),
-                        bank[:].rearrange("p t j -> p j t"),
-                        woven[:],
-                        MULT,
-                    )
+                d = bank[:].rearrange("p t j -> p j t")
+                woven = ring.tile([P, BANK_J, PACK], F32, name="stiff_woven", bufs=4)
+                nc.scalar.copy(out=woven[:], in_=stiff_sb[b, g][:, :, lo : lo + BANK_J].rearrange("p t j -> p j t"))
+                product = ring.tile([P, BANK_J, PACK], F32, name="product", bufs=6)
+                if on_vector:
+                    nc.vector.tensor_tensor(product[:], d, woven[:], MULT)
                 else:
-                    sq = ring.tile([P, BANK_J // 2, PACK, 2], F32, name="sq")
-                    nc.scalar.activation(sq[:], bank[:].rearrange("p t (c i) -> p c t i", i=2), SQUARE)
-                    nc.gpsimd.tensor_tensor(
-                        mid[:].rearrange("p (c t i) -> p c t i", t=PACK, i=2),
-                        sq[:],
-                        stiff_rows.rearrange("p t (c i) -> p c t i", i=2),
-                        MULT,
-                    )
-                banks.append(bank)
-                mids.append(mid)
-            for s in range(width // BANK_J):
-                h_part = h_bf[:, BANK * s : BANK * (s + 1)]
-                if s < vector_banks:
-                    nc.vector.scalar_tensor_tensor(
-                        h_part.rearrange("p (j t) -> p j t", t=PACK),
-                        mids[s][:].rearrange("p (j t) -> p j t", t=PACK),
-                        1.0,
-                        banks[s][:].rearrange("p t j -> p j t"),
-                        ADD,
-                        MULT,
-                    )
+                    square = ring.tile([P, BANK_J, PACK], F32, name="square")
+                    nc.scalar.activation(square[:], d, SQUARE)
+                    nc.gpsimd.tensor_tensor(product[:], square[:], woven[:], MULT)
+                pending.append((d, product))
+            for s, (d, product) in enumerate(pending):
+                h_part = h_bf[b, g][:, BANK * s : BANK * (s + 1)].rearrange("p (j t) -> p j t", t=PACK)
+                if on_vector:
+                    nc.vector.scalar_tensor_tensor(h_part, product[:], 1.0, d, ADD, MULT)
                 else:
-                    nc.vector.tensor_tensor(
-                        h_part.rearrange("p (c i t) -> p c i t", i=2, t=PACK),
-                        banks[s][:].rearrange("p t (c i) -> p c i t", i=2),
-                        mids[s][:].rearrange("p (c t i) -> p c i t", t=PACK, i=2),
-                        ADD,
-                    )
+                    nc.vector.tensor_tensor(h_part, d, product[:], ADD)
 
-        def quantise_h(b, g, h_bf):
+        def quantise_h(b, g):
             width = GROUPS[g][1]
             h_codes[b, g] = keep.tile([P, width], U32, name=f"h_codes{b}{g}", align_bytes=64)
             h_sc[b, g] = keep.tile([P, width], U8, name=f"h_sc{b}{g}", align_bytes=64)
-            nc.vector.quantize_mx(out=h_codes[b, g][:].bitcast(FP8X4), scales=h_sc[b, g][:], in_=h_bf[:])
+            nc.vector.quantize_mx(out=h_codes[b, g][:].bitcast(FP8X4), scales=h_sc[b, g][:], in_=h_bf[b, g][:])
 
         def make_y(g):
             width = GROUPS[g][1]
             per_bank = BANK // width
-            step = BANK if width == BANK else BANK_J
+            moving = BANK if width == BANK else P
             ys = []
-            for first in range(0, 4, per_bank):
+            for first in range(0, N_TILES, per_bank):
                 bank = psum_y.tile([P, per_bank, width], F32, name="y_bank")
-                for qq in range(per_bank):
-                    q = first + qq
-                    for lo in range(0, width, step):
-                        cols = slice(lo, lo + step)
-                        for b in range(2):
+                for i in range(per_bank):
+                    q = first + i
+                    for lo in range(0, width, moving):
+                        cols = slice(lo, lo + moving)
+                        for b in range(PASSES):
                             nc.tensor.matmul_mx(
-                                out=bank[:, qq, cols],
+                                out=bank[:, i, cols],
                                 lhsT=w4_sb[:, b, 2 * P * q : 2 * P * (q + 1)].bitcast(FP4X4),
                                 lhsT_scale=w4_sc[:, b, P * q : P * (q + 1)],
                                 rhs=h_codes[b, g][:, cols].bitcast(FP8X4),
                                 rhs_scale=h_sc[b, g][:, cols],
                                 start=(b == 0),
-                                stop=(b == 1),
+                                stop=(b == PASSES - 1),
                             )
-                y_neg = ring.tile([P, per_bank, width], F32, name="y_neg", bufs=4)
+                y_neg = ring.tile([P, per_bank, width], F32, name="y_neg", bufs=N_TILES)
                 nc.scalar.activation(y_neg[:], bank[:], COPY, scale=-1.0)
-                ys.extend([y_neg[:, qq, :] for qq in range(per_bank)])
+                ys.extend([y_neg[:, i, :] for i in range(per_bank)])
             return ys
 
-        z_sb = [keep.tile([P, S], F32, name=f"z{q}") for q in range(4)]
+        weighted = [keep.tile([P, S], F32, name=f"weighted{q}") for q in range(N_TILES)]
 
-        def make_z(g, ys):
+        def weigh(g, ys):
             j0, width = GROUPS[g]
-            for q in range(4):
-                nc.gpsimd.tensor_tensor(z_sb[q][:, j0 : j0 + width], ys[q], wgo_sb[:, j0 : j0 + width], MULT)
+            for q in range(N_TILES):
+                nc.gpsimd.tensor_tensor(weighted[q][:, j0 : j0 + width], ys[q], wgo_sb[:, j0 : j0 + width], MULT)
 
-        pages = {q: keep.tile([P, S], F32, name=f"page{q}") for q in range(3)}
+        last = N_TILES - 1
+        pages = {q: keep.tile([P, S], F32, name=f"page{q}") for q in range(last)}
 
         def scatter(q, j0, width):
-            nc.vector.tensor_copy(
-                pages[q][:].indirect(offs2_sb[:, j0 // 16 : (j0 + width) // 16]), z_sb[q][:, j0 : j0 + width]
-            )
+            entries = offs2_sb[:, j0 // PER_COL : (j0 + width) // PER_COL]
+            nc.vector.tensor_copy(pages[q][:].indirect(entries), weighted[q][:, j0 : j0 + width])
 
-        def finish(q, on_vector):
-            for half in range(2):
-                cols = slice(BANK * half, BANK * (half + 1))
+        def finish(q):
+            for lo in range(0, S, BANK):
+                cols = slice(lo, lo + BANK)
                 res = ring.tile([P, BANK], F32, name="res")
-                if on_vector:
+                if q == last:
                     nc.vector.scalar_tensor_tensor(res[:], pages[q][:, cols], 1.0, x0_sb[:, q, cols], ADD, MULT)
                 else:
                     factor = ring.tile([P, BANK], F32, name="factor", bufs=2)
                     nc.scalar.activation(factor[:], pages[q][:, cols], COPY, bias=1.0)
                     nc.gpsimd.tensor_tensor(res[:], factor[:], x0_sb[:, q, cols], MULT)
-                queue = nc.scalar if on_vector else nc.sync
+                queue = nc.scalar if q == last else nc.sync
                 queue.dma_start(out=out[P * q : P * (q + 1), cols], in_=res[:])
 
-        h_bf = {}
-        for b in range(2):
-            for g in range(2):
-                h_bf[b, g] = keep.tile([P, PACK * GROUPS[g][1]], BF16, name=f"h_bf{b}{g}", align_bytes=64)
-        h_bf[0, 2] = keep.tile([P, PACK * GROUPS[2][1]], BF16, name="h_bf02", align_bytes=64)
-        h_bf[1, 2] = shared.tile([P, PACK * GROUPS[2][1]], BF16, name="h_bf12", align_bytes=64, offset=0)
-
-        make_h(0, 0, 2, h_bf[0, 0])
-        make_h(1, 0, 2, h_bf[1, 0])
-        quantise_h(0, 0, h_bf[0, 0])
-        quantise_h(1, 0, h_bf[1, 0])
-        y0 = make_y(0)
-        make_h(0, 1, 2, h_bf[0, 1])
-        make_h(1, 1, 0, h_bf[1, 1])
-        quantise_h(0, 1, h_bf[0, 1])
-        quantise_h(1, 1, h_bf[1, 1])
-        make_z(0, y0)
-        y1 = make_y(1)
-        for q in range(3):
-            scatter(q, 0, 256)
-        make_h(0, 2, 0, h_bf[0, 2])
-        quantise_h(0, 2, h_bf[0, 2])
-        make_z(1, y1)
-        for q in range(3):
-            scatter(q, 256, 256)
-        make_h(1, 2, 0, h_bf[1, 2])
-        quantise_h(1, 2, h_bf[1, 2])
-        pages[3] = shared.tile([P, S], F32, name="page3", align_bytes=64, offset=0)
-        scatter(3, 0, 512)
-        make_z(2, make_y(2))
-        for q in range(4):
-            scatter(q, 512, 512)
-            finish(q, q == 3)
+        make_h(0, 0, keep)
+        make_h(1, 0, keep)
+        quantise_h(0, 0)
+        quantise_h(1, 0)
+        ys0 = make_y(0)
+        make_h(0, 1, keep)
+        make_h(1, 1, keep)
+        quantise_h(0, 1)
+        quantise_h(1, 1)
+        weigh(0, ys0)
+        ys1 = make_y(1)
+        for q in range(last):
+            scatter(q, *GROUPS[0])
+        make_h(0, 2, keep)
+        quantise_h(0, 2)
+        weigh(1, ys1)
+        for q in range(last):
+            scatter(q, *GROUPS[1])
+        make_h(1, 2, shared, offset=0)
+        quantise_h(1, 2)
+        pages[last] = shared.tile([P, S], F32, name="page_last", align_bytes=64, offset=0)
+        scatter(last, 0, GROUPS[2][0])
+        weigh(2, make_y(2))
+        for q in range(N_TILES):
+            scatter(q, *GROUPS[2])
+            finish(q)

@@ -59,6 +59,19 @@ def tile_list_kidney_mesh_stress_kernel(
             w1_raw[a] = keep.tile([P, PACK, H], F32, name=f"w1_raw{a}")
             nc.sync.dma_start(out=w1_raw[a][:], in_=w1[KP * a : KP * (a + 1), :].rearrange("(p j) c -> p j c", j=PACK))
 
+        def load_w1_rows(half):
+            rows = slice(2 * half, 2 * half + 2)
+            nc.sync.dma_start(
+                out=w1_raw[0][:, rows, :], in_=w1[0:KP, :].rearrange("(p j) c -> p j c", j=PACK)[:, rows, :]
+            )
+
+        def load_tab_scales(n):
+            a, q = divmod(n, 4)
+            nc.sync.dma_start(
+                out=tab_sc[32 * q + 4 * a : 32 * q + 4 * a + 4, :].bitcast(I32),
+                in_=tab_scales[a, 4 * q : 4 * q + 4, :].bitcast(I32),
+            )
+
         def load_tab(a):
             tab_sb[a] = keep.tile([P, T], U32, name=f"tab{a}")
             nc.sync.dma_start(
@@ -74,13 +87,14 @@ def tile_list_kidney_mesh_stress_kernel(
                 in_=stiff[KP * b : KP * (b + 1), j0 : j0 + width].rearrange("(p t) j -> p t j", t=PACK),
             )
 
+        w1_raw[0] = keep.tile([P, PACK, H], F32, name="w1_raw0")
+        load_w1_rows(0)
+        for n in range(6):
+            load_tab_scales(n)
+        load_w1_rows(1)
+        for n in range(6, 8):
+            load_tab_scales(n)
         nc.sync.dma_start(offs_sb[:], offs)
-        load_w1(0)
-        for q in range(4):
-            nc.sync.dma_start(
-                out=tab_sc[32 * q : 32 * q + 4 * PASSES, :].bitcast(I32),
-                in_=tab_scales[:, 4 * q : 4 * q + 4, :].bitcast(I32),
-            )
         load_w1(1)
         load_tab(0)
         load_tab(1)

@@ -59,12 +59,6 @@ def tile_list_kidney_mesh_stress_kernel(
             w1_raw[a] = keep.tile([P, PACK, H], F32, name=f"w1_raw{a}")
             nc.sync.dma_start(out=w1_raw[a][:], in_=w1[KP * a : KP * (a + 1), :].rearrange("(p j) c -> p j c", j=PACK))
 
-        def load_w1_rows(half):
-            rows = slice(2 * half, 2 * half + 2)
-            nc.sync.dma_start(
-                out=w1_raw[0][:, rows, :], in_=w1[0:KP, :].rearrange("(p j) c -> p j c", j=PACK)[:, rows, :]
-            )
-
         def load_tab_scales(n):
             a, q = divmod(n, 4)
             nc.sync.dma_start(
@@ -87,15 +81,13 @@ def tile_list_kidney_mesh_stress_kernel(
                 in_=stiff[KP * b : KP * (b + 1), j0 : j0 + width].rearrange("(p t) j -> p t j", t=PACK),
             )
 
-        w1_raw[0] = keep.tile([P, PACK, H], F32, name="w1_raw0")
-        load_w1_rows(0)
-        for n in range(6):
-            load_tab_scales(n)
-        load_w1_rows(1)
-        for n in range(6, 8):
-            load_tab_scales(n)
         nc.sync.dma_start(offs_sb[:], offs)
+        load_w1(0)
+        for n in range(5):
+            load_tab_scales(n)
         load_w1(1)
+        for n in range(5, 8):
+            load_tab_scales(n)
         load_tab(0)
         load_tab(1)
         for g in range(2):
@@ -159,16 +151,16 @@ def tile_list_kidney_mesh_stress_kernel(
                 lo = BANK_J * s
                 half, jh = divmod(j0 + lo, HALF)
                 bank = psum_d.tile([P, PACK, BANK_J], F32, name="d_bank")
-                for t in range(PACK):
-                    for a in range(PASSES):
+                for a in range(PASSES):
+                    for t in range(PACK):
                         nc.tensor.matmul_mx(
                             out=bank[:, t, :],
                             lhsT=w1_codes[a, b][:, P * t : P * (t + 1)].bitcast(FP8X4),
                             lhsT_scale=w1_sc[a, b][:, P * t : P * (t + 1)],
                             rhs=v_words[a, half][:, jh : jh + BANK_J].bitcast(FP8X4),
                             rhs_scale=v_sc[4 * a :, j0 + lo : j0 + lo + BANK_J],
-                            start=(a == 0),
-                            stop=(a == PASSES - 1),
+                            start=(a == 0 and t == 0),
+                            stop=(a == PASSES - 1 and t == PACK - 1),
                         )
                 d = bank[:].rearrange("p t j -> p j t")
                 woven = ring.tile([P, BANK_J, PACK], F32, name="stiff_woven", bufs=4)

@@ -144,11 +144,11 @@ def tile_list_kidney_mesh_stress_kernel(
 
         def make_h(b, g, pool, **place):
             j0, width = GROUPS[g]
-            on_vector = (b, g) in VECTOR_PIECES
             h_bf[b, g] = pool.tile([P, PACK * width], BF16, name=f"h_bf{b}{g}", align_bytes=64, **place)
             pending = []
             for s in range(width // BANK_J):
                 lo = BANK_J * s
+                on_vector = (b, g) in VECTOR_PIECES or ((b, g) == (1, 2) and s >= 2)
                 half, jh = divmod(j0 + lo, HALF)
                 bank = psum_d.tile([P, PACK, BANK_J], F32, name="d_bank")
                 for a in range(PASSES):
@@ -172,8 +172,8 @@ def tile_list_kidney_mesh_stress_kernel(
                     square = ring.tile([P, BANK_J, PACK], F32, name="square")
                     nc.scalar.activation(square[:], d, SQUARE)
                     nc.gpsimd.tensor_tensor(product[:], square[:], woven[:], MULT)
-                pending.append((d, product))
-            for s, (d, product) in enumerate(pending):
+                pending.append((d, product, on_vector))
+            for s, (d, product, on_vector) in enumerate(pending):
                 h_part = h_bf[b, g][:, BANK * s : BANK * (s + 1)].rearrange("p (j t) -> p j t", t=PACK)
                 if on_vector:
                     nc.vector.scalar_tensor_tensor(h_part, product[:], 1.0, d, ADD, MULT)

from contextlib import ExitStack

import concourse.mybir as mybir

K, H, N, T, S = 1024, 1024, 512, 4096, 1024
FLOPS = 2 * K * H * S + 2 * H * N * S

F32 = mybir.dt.float32
BF16 = mybir.dt.bfloat16
I32 = mybir.dt.int32
U32 = mybir.dt.uint32
U16 = mybir.dt.uint16
U8 = mybir.dt.uint8
FP8X4 = mybir.dt.float8_e4m3fn_x4
FP4X4 = mybir.dt.float4_e2m1fn_x4
MULT = mybir.AluOpType.mult
ADD = mybir.AluOpType.add
COPY = mybir.ActivationFunctionType.Copy
SQUARE = mybir.ActivationFunctionType.Square

P = 128
PACK = 4
KP = P * PACK
PASSES = K // KP
N_TILES = N // P
BANK = 512
BANK_J = BANK // PACK
PER_COL = 16
HALF = S // 2
GROUPS = [(0, 256), (256, 256), (512, 512)]
VECTOR_PIECES = [(0, 0), (1, 0), (0, 1)]


def tile_list_kidney_mesh_stress_kernel(
    tc, tab_words, tab_scales, offs, w1, stiff, w4_words, w4_scales, offs2, wgo, x0, out
):
    nc = tc.nc

    with ExitStack() as ctx:
        keep = ctx.enter_context(tc.tile_pool(name="keep", bufs=1))
        ring = ctx.enter_context(tc.tile_pool(name="ring", bufs=3))
        shared = ctx.enter_context(tc.tile_pool(name="shared", bufs=1))
        psum_d = ctx.enter_context(tc.psum_pool(name="psum_d", bufs=6))
        psum_y = ctx.enter_context(tc.psum_pool(name="psum_y", bufs=2))

        offs_sb = keep.tile([P, S // PER_COL], U16, name="offs_sb")
        offs2_sb = keep.tile([P, S // PER_COL], U16, name="offs2_sb")

        tab_sc = keep.tile([P, T], U8, name="tab_sc", align_bytes=64)
        w4_sc = keep.tile([P, PASSES, N], U8, name="w4_sc", align_bytes=64)
        nc.vector.memset(tab_sc[:].bitcast(I32), 0)
        nc.vector.memset(w4_sc[:].rearrange("p a n -> p (a n)").bitcast(I32), 0)

        w1_raw = {}
        tab_sb = {}
        stiff_sb = {}

        def load_w1(a):
            w1_raw[a] = keep.tile([P, PACK, H], F32, name=f"w1_raw{a}")
            nc.sync.dma_start(out=w1_raw[a][:], in_=w1[KP * a : KP * (a + 1), :].rearrange("(p j) c -> p j c", j=PACK))

        def load_tab_scales(n):
            a, q = divmod(n, 4)
            nc.sync.dma_start(
                out=tab_sc[32 * q + 4 * a : 32 * q + 4 * a + 4, :].bitcast(I32),
                in_=tab_scales[a, 4 * q : 4 * q + 4, :].bitcast(I32),
            )

        def load_tab(a):
            tab_sb[a] = keep.tile([P, T], U32, name=f"tab{a}")
            nc.sync.dma_start(
                out=tab_sb[a][:].bitcast(I32),
                in_=tab_words[a].rearrange("p n t -> p (n t)").bitcast(I32),
            )

        def load_stiff(b, g):
            j0, width = GROUPS[g]
            stiff_sb[b, g] = keep.tile([P, PACK, width], F32, name=f"stiff{b}{g}")
            nc.sync.dma_start(
                out=stiff_sb[b, g][:],
                in_=stiff[KP * b : KP * (b + 1), j0 : j0 + width].rearrange("(p t) j -> p t j", t=PACK),
            )

        nc.sync.dma_start(offs_sb[:], offs)
        load_w1(0)
        for n in range(5):
            load_tab_scales(n)
        load_w1(1)
        for n in range(5, 8):
            load_tab_scales(n)
        load_tab(0)
        load_tab(1)
        for g in range(2):
            for b in range(PASSES):
                load_stiff(b, g)
        w4_sb = keep.tile([P, PASSES, 2 * N], U8, name="w4_sb", align_bytes=64)
        nc.sync.dma_start(out=w4_sb[:].bitcast(I32), in_=w4_words.rearrange("a p n -> p a n").bitcast(I32))
        for q in range(4):
            nc.sync.dma_start(
                out=w4_sc[32 * q : 32 * q + 4, :, :].bitcast(I32),
                in_=w4_scales[:, 4 * q : 4 * q + 4, :].rearrange("a r n -> r a n").bitcast(I32),
            )
        wgo_sb = keep.tile([P, S], F32, name="wgo_sb")
        nc.sync.dma_start(out=wgo_sb[:], in_=wgo)
        nc.sync.dma_start(offs2_sb[:], offs2)
        for b in range(PASSES):
            load_stiff(b, 2)

        w1_codes = {}
        w1_sc = {}

        def quantise_w1(a, b):
            grouped = ring.tile([P, KP * PACK], BF16, name="w1_bf", align_bytes=64)
            dst = grouped[:].rearrange("p (t m j) -> p m t j", t=PACK, j=PACK)
            src = w1_raw[a][:, :, KP * b : KP * (b + 1)].rearrange("p j (m t) -> p m t j", t=PACK)
            if (a, b) == (1, 0):
                nc.vector.tensor_copy(out=dst, in_=src)
            else:
                nc.scalar.copy(out=dst, in_=src)
            w1_codes[a, b] = keep.tile([P, KP], U32, name=f"w1_codes{a}{b}", align_bytes=64)
            w1_sc[a, b] = keep.tile([P, KP], U8, name=f"w1_sc{a}{b}", align_bytes=64)
            nc.vector.quantize_mx(out=w1_codes[a, b][:].bitcast(FP8X4), scales=w1_sc[a, b][:], in_=grouped[:])

        v_sc = keep.tile([P, S], U8, name="v_sc", align_bytes=64)
        nc.vector.tensor_copy(v_sc[:], tab_sc[:].indirect(offs_sb[:]))
        for a in range(PASSES):
            for b in range(PASSES):
                quantise_w1(a, b)

        x0_sb = w1_raw[0]
        for q in range(N_TILES):
            nc.sync.dma_start(out=x0_sb[:, q, :], in_=x0[P * q : P * (q + 1), :])

        v_words = {}
        for a in range(PASSES):
            for half in range(2):
                v_words[a, half] = keep.tile([P, HALF], U32, name=f"v_words{a}{half}", align_bytes=64)
                entries = offs_sb[:, HALF * half // PER_COL : HALF * (half + 1) // PER_COL]
                nc.vector.tensor_copy(v_words[a, half][:], tab_sb[a][:].indirect(entries))

        h_bf = {}
        h_codes = {}
        h_sc = {}

        def make_h(b, g, pool, **place):
            j0, width = GROUPS[g]
            h_bf[b, g] = pool.tile([P, PACK * width], BF16, name=f"h_bf{b}{g}", align_bytes=64, **place)
            pending = []
            for s in range(width // BANK_J):
                lo = BANK_J * s
                on_vector = (b, g) in VECTOR_PIECES or ((b, g) == (1, 2) and s >= 2)
                half, jh = divmod(j0 + lo, HALF)
                bank = psum_d.tile([P, PACK, BANK_J], F32, name="d_bank")
                for a in range(PASSES):
                    for t in range(PACK):
                        nc.tensor.matmul_mx(
                            out=bank[:, t, :],
                            lhsT=w1_codes[a, b][:, P * t : P * (t + 1)].bitcast(FP8X4),
                            lhsT_scale=w1_sc[a, b][:, P * t : P * (t + 1)],
                            rhs=v_words[a, half][:, jh : jh + BANK_J].bitcast(FP8X4),
                            rhs_scale=v_sc[4 * a :, j0 + lo : j0 + lo + BANK_J],
                            start=(a == 0 and t == 0),
                            stop=(a == PASSES - 1 and t == PACK - 1),
                        )
                d = bank[:].rearrange("p t j -> p j t")
                woven = ring.tile([P, BANK_J, PACK], F32, name="stiff_woven", bufs=4)
                nc.scalar.copy(out=woven[:], in_=stiff_sb[b, g][:, :, lo : lo + BANK_J].rearrange("p t j -> p j t"))
                product = ring.tile([P, BANK_J, PACK], F32, name="product", bufs=6)
                if on_vector:
                    nc.vector.tensor_tensor(product[:], d, woven[:], MULT)
                else:
                    square = ring.tile([P, BANK_J, PACK], F32, name="square")
                    nc.scalar.activation(square[:], d, SQUARE)
                    nc.gpsimd.tensor_tensor(product[:], square[:], woven[:], MULT)
                pending.append((d, product, on_vector))
            for s, (d, product, on_vector) in enumerate(pending):
                h_part = h_bf[b, g][:, BANK * s : BANK * (s + 1)].rearrange("p (j t) -> p j t", t=PACK)
                if on_vector:
                    nc.vector.scalar_tensor_tensor(h_part, product[:], 1.0, d, ADD, MULT)
                else:
                    nc.vector.tensor_tensor(h_part, d, product[:], ADD)

        def quantise_h(b, g):
            width = GROUPS[g][1]
            h_codes[b, g] = keep.tile([P, width], U32, name=f"h_codes{b}{g}", align_bytes=64)
            h_sc[b, g] = keep.tile([P, width], U8, name=f"h_sc{b}{g}", align_bytes=64)
            nc.vector.quantize_mx(out=h_codes[b, g][:].bitcast(FP8X4), scales=h_sc[b, g][:], in_=h_bf[b, g][:])

        def make_y(g):
            width = GROUPS[g][1]
            per_bank = BANK // width
            moving = BANK if width == BANK else P
            ys = []
            for first in range(0, N_TILES, per_bank):
                bank = psum_y.tile([P, per_bank, width], F32, name="y_bank")
                for i in range(per_bank):
                    q = first + i
                    for lo in range(0, width, moving):
                        cols = slice(lo, lo + moving)
                        for b in range(PASSES):
                            nc.tensor.matmul_mx(
                                out=bank[:, i, cols],
                                lhsT=w4_sb[:, b, 2 * P * q : 2 * P * (q + 1)].bitcast(FP4X4),
                                lhsT_scale=w4_sc[:, b, P * q : P * (q + 1)],
                                rhs=h_codes[b, g][:, cols].bitcast(FP8X4),
                                rhs_scale=h_sc[b, g][:, cols],
                                start=(b == 0),
                                stop=(b == PASSES - 1),
                            )
                y_neg = ring.tile([P, per_bank, width], F32, name="y_neg", bufs=N_TILES)
                nc.scalar.activation(y_neg[:], bank[:], COPY, scale=-1.0)
                ys.extend([y_neg[:, i, :] for i in range(per_bank)])
            return ys

        weighted = [keep.tile([P, S], F32, name=f"weighted{q}") for q in range(N_TILES)]

        def weigh(g, ys):
            j0, width = GROUPS[g]
            for q in range(N_TILES):
                nc.gpsimd.tensor_tensor(weighted[q][:, j0 : j0 + width], ys[q], wgo_sb[:, j0 : j0 + width], MULT)

        last = N_TILES - 1
        pages = {q: keep.tile([P, S], F32, name=f"page{q}") for q in range(last)}

        def scatter(q, j0, width):
            entries = offs2_sb[:, j0 // PER_COL : (j0 + width) // PER_COL]
            nc.vector.tensor_copy(pages[q][:].indirect(entries), weighted[q][:, j0 : j0 + width])

        def finish(q):
            for lo in range(0, S, BANK):
                cols = slice(lo, lo + BANK)
                res = ring.tile([P, BANK], F32, name="res")
                if q == last:
                    nc.vector.scalar_tensor_tensor(res[:], pages[q][:, cols], 1.0, x0_sb[:, q, cols], ADD, MULT)
                else:
                    factor = ring.tile([P, BANK], F32, name="factor", bufs=2)
                    nc.scalar.activation(factor[:], pages[q][:, cols], COPY, bias=1.0)
                    nc.gpsimd.tensor_tensor(res[:], factor[:], x0_sb[:, q, cols], MULT)
                queue = nc.scalar if q == last else nc.sync
                queue.dma_start(out=out[P * q : P * (q + 1), cols], in_=res[:])

        make_h(0, 0, keep)
        make_h(1, 0, keep)
        quantise_h(0, 0)
        quantise_h(1, 0)
        ys0 = make_y(0)
        make_h(0, 1, keep)
        make_h(1, 1, keep)
        quantise_h(0, 1)
        quantise_h(1, 1)
        weigh(0, ys0)
        ys1 = make_y(1)
        for q in range(last):
            scatter(q, *GROUPS[0])
        make_h(0, 2, keep)
        quantise_h(0, 2)
        weigh(1, ys1)
        for q in range(last):
            scatter(q, *GROUPS[1])
        make_h(1, 2, shared, offset=0)
        quantise_h(1, 2)
        pages[last] = shared.tile([P, S], F32, name="page_last", align_bytes=64, offset=0)
        scatter(last, 0, GROUPS[2][0])
        weigh(2, make_y(2))
        for q in range(N_TILES):
            scatter(q, *GROUPS[2])
            finish(q)
